import numpy as np, ml_dtypes
CORES = [21,85,149,213,277,341,405,469]
N = 8
C = 128
SIGN = [[1,1,1,1,1,1,1,1],[1,-1,1,-1,1,-1,1,-1],[1,1,-1,-1,1,1,-1,-1],[1,-1,-1,1,1,-1,-1,1],[1,1,1,1,-1,-1,-1,-1],[1,-1,1,-1,-1,1,-1,1],[1,1,-1,-1,-1,-1,1,1],[1,-1,-1,1,-1,1,1,-1]]
def setup_inputs(rng):
    return {"x": rng.standard_normal((N, 128, C), dtype=np.float32).astype(ml_dtypes.bfloat16), "w": (rng.standard_normal((N, 128, 128), dtype=np.float32) / 11).astype(ml_dtypes.bfloat16)}
def setup_inputs_big(rng):
    d = setup_inputs(rng)
    for k in ("x", "w"): d[k] = (d[k].astype(np.float32) * 1024.0).astype(d[k].dtype)
    return d
def setup_inputs_small(rng):
    d = setup_inputs(rng)
    for k in ("x", "w"): d[k] = (d[k].astype(np.float32) * (1 / 1024.0)).astype(d[k].dtype)
    return d
def setup_inputs_apart(rng):
    d = setup_inputs(rng)
    f = (10.0 ** rng.permutation(np.linspace(-1.5, 1.5, N))).astype(np.float32).reshape(N, 1, 1)
    for k in ("x", "w"): d[k] = (d[k].astype(np.float32) * f).astype(d[k].dtype)
    return d
def reference(x, w):
    X = x.astype(np.float64)
    y = np.stack([w[r].astype(np.float64).T @ sum(SIGN[r][j] * X[j] for j in range(N)) for r in range(N)])
    return {"y": y.astype(ml_dtypes.bfloat16)}

from concourse.bass import DstId, RemoteDMATransfer
from concourse.mybir import AluOpType

_B = "bfloat16"
SCRATCH = {
    "xd": ("dram", [128, 128], _B),
    "xpd": ("dram", [128, 128], _B),
    "xs": ("sbuf", [128, 128], _B),
    "ws": ("sbuf", [128, 128], _B),
    "zero": ("sbuf", [128, 128], _B),
    "negx": ("sbuf", [128, 128], _B),
    "negw": ("sbuf", [128, 128], _B),
    "xp": ("sbuf", [128, 128], _B),
    "raw0": ("sbuf", [128, 128], _B),
    "raw1": ("sbuf", [128, 128], _B),
    "pair0": ("sbuf", [128, 128], _B),
    "pair1": ("sbuf", [128, 128], _B),
    "ysb": ("sbuf", [128, 128], _B),
    "acc": ("psum", [128, 128], "float32"),
}
SEMAPHORES = ["ld_xd", "ld_xs", "ld_w", "zs", "nx", "nw", "arr_p", "ld_xp", "arr_raw", "arr_pair0", "arr_pair1",
              "mm", "cp", "st", "sent"]

ENGINES_1A = 4


def _bits(mask):
    return [b for b in range(mask.bit_length()) if (mask >> b) & 1]


def _count(mask):
    return len(_bits(mask))


def _lowest(mask, k):
    return sum(1 << b for b in _bits(mask)[:k])


def _mask_all(topo, cores, j, ds):
    m = topo.mask(cores[j], cores[ds[0]])
    for d in ds[1:]:
        m &= topo.mask(cores[j], cores[d])
    return m


def _plan(cores, topo):
    n = len(cores)
    partner, pair_to, raw_to = {}, {}, {}
    for r, c in enumerate(cores):
        partner[r] = [j for j, cj in enumerate(cores)
                      if topo.rack(topo.host(cj)) != topo.rack(topo.host(c)) and topo.chip(cj) == topo.chip(c)
                      and topo.may_write(c, cj)][0]
    for r, c in enumerate(cores):
        p = partner[r]
        reach = [d for d in range(n) if d not in (r, p) and topo.may_write(c, cores[d])]
        pair_to[r] = [d for d in reach if not topo.may_write(cores[p], cores[d])]
        raw_to[r] = [d for d in reach if d not in pair_to[r]]
    return partner, pair_to, raw_to


def rank_program(g, core, T, topo):
    rank = T.rank_of(core)
    if rank is None:
        return
    cores, sign, sem = list(T.cores), T.tables["SIGN"], T.sem
    n = len(cores)
    partner, pair_to, raw_to = _plan(cores, topo)
    p = partner[rank]
    raw_from = {d: [j for j in range(n) if d in raw_to[j]] for d in range(n)}
    pair_from = {d: [j for j in range(n) if d in pair_to[j]] for d in range(n)}

    def dst_id(d):
        rid, pid = topo.addr(cores[d], core)
        return DstId(rid=rid, pnc=pid)

    groups = {}
    for d in pair_to[rank]:
        groups.setdefault((sign[d][rank] * sign[d][p], pair_from[d].index(rank)), []).append(d)
    need_negx = any(rel < 0 for rel, _ in groups)

    raw_total = sum(_count(_mask_all(topo, cores, j, raw_to[j])) for j in raw_from[rank])
    arr_p_total = _count(_lowest(topo.mask(cores[p], core), ENGINES_1A))
    terms = [(sign[rank][rank], T.xs, None, 0)]
    for k, j in enumerate(raw_from[rank]):
        terms.append((sign[rank][j], T["raw%d" % k], sem.arr_raw, raw_total))
    terms.append((sign[rank][p], T.xp, sem.ld_xp, 16))
    for k, j in enumerate(pair_from[rank]):
        terms.append((sign[rank][partner[j]], T["pair%d" % k], sem["arr_pair%d" % k],
                      _count(_mask_all(topo, cores, j, pair_to[j]))))
    need_negw = any(s < 0 for s, _, _, _ in terms)

    g.sync.dma_start(T.xd[:], T.x[:]).then_inc(sem.ld_xd, 16)
    g.sync.dma_start(T.xs[:], T.x[:]).then_inc(sem.ld_xs, 16)
    g.sync.dma_start(T.ws[:], T.w[:]).then_inc(sem.ld_w, 16)

    if need_negx or need_negw:
        g.vector.memset(T.zero[:], 0.0).then_inc(sem.zs, 1)
        g.vector.wait_ge(sem.zs, 1)
    if need_negx:
        g.vector.wait_ge(sem.ld_xs, 16)
        g.vector.tensor_tensor(T.negx[:], T.zero[:], T.xs[:], AluOpType.subtract).then_inc(sem.nx, 1)
    if need_negw:
        g.vector.wait_ge(sem.ld_w, 16)
        g.vector.tensor_tensor(T.negw[:], T.zero[:], T.ws[:], AluOpType.subtract).then_inc(sem.nw, 1)

    sent = 0
    m1a = _lowest(topo.mask(core, cores[p]), ENGINES_1A)
    rid, pid = topo.addr(cores[p], core)
    g.wait_ge(sem.ld_xd, 16)
    g.remote_dma(out_ap=T.xpd[:], in_ap=T.xd[:], remote_sem=sem.arr_p, local_sem=sem.sent, pid=pid, routing_id=rid,
                 dma_engine_mask=m1a)
    sent += _count(m1a)

    g.wait_ge(sem.ld_xs, 16)
    m1b = _mask_all(topo, cores, rank, raw_to[rank])
    g.remote_dma_fused([RemoteDMATransfer(
        dst_ids=[dst_id(d) for d in raw_to[rank]], dma_engine_mask=m1b, remote_sem=sem.arr_raw, srcs=[T.xs[:]],
        dsts=[T["raw%d" % raw_from[d].index(rank)][:] for d in raw_to[rank]], alu_op=0)], local_sem=sem.sent)
    sent += _count(m1b)

    g.wait_ge(sem.arr_p, arr_p_total)
    if need_negx:
        g.wait_ge(sem.nx, 1)
    m2 = _mask_all(topo, cores, rank, pair_to[rank])
    for (rel, slot), ds in sorted(groups.items()):
        own = T.xs if rel > 0 else T.negx
        g.remote_dma_fused([RemoteDMATransfer(
            dst_ids=[dst_id(d) for d in ds], dma_engine_mask=m2, remote_sem=sem["arr_pair%d" % slot],
            srcs=[T.xpd[:], own[:]], dsts=[T["pair%d" % slot][:] for d in ds], alu_op=1)], local_sem=sem.sent)
        sent += _count(m2)

    g.sync.wait_ge(sem.arr_p, arr_p_total)
    g.sync.dma_start(T.xp[:], T.xpd[:]).then_inc(sem.ld_xp, 16)

    g.tensor.wait_ge(sem.ld_xs, 16)
    g.tensor.wait_ge(sem.ld_w, 16)
    if need_negw:
        g.tensor.wait_ge(sem.nw, 1)
    last = len(terms) - 1
    for i, (s, buf, wsem, cnt) in enumerate(terms):
        if wsem is not None:
            g.tensor.wait_ge(wsem, cnt)
        mm = g.tensor.matmul(T.acc[:], (T.ws if s > 0 else T.negw)[:], buf[:], i == 0, i == last)
        if i == last:
            mm.then_inc(sem.mm, 1)

    g.vector.wait_ge(sem.mm, 1)
    g.vector.tensor_copy(T.ysb[:], T.acc[:]).then_inc(sem.cp, 1)
    g.sync.wait_ge(sem.cp, 1)
    g.sync.dma_start(T.y[:], T.ysb[:]).then_inc(sem.st, 16)
    g.sync.wait_ge(sem.st, 16)
    g.wait_ge(sem.sent, sent)
